import numpy as np
import ml_dtypes


def mxq(x, axis, fmt="e4m3"):
    dtype, down = {"e4m3": (ml_dtypes.float8_e4m3fn, 7), "e5m2": (ml_dtypes.float8_e5m2, 14)}[fmt]
    v = np.moveaxis(np.asarray(x, np.float32).astype(ml_dtypes.bfloat16).astype(np.float64), axis, -1)
    blocks = v.reshape(v.shape[:-1] + (-1, 32))
    amax = np.abs(blocks).max(-1, keepdims=True)
    byte = np.maximum(np.where(amax > 0, np.frexp(amax)[1] - 1 + 127, 0) - down, 1)
    scale = np.exp2(byte - 127.0)
    codes = (blocks / scale).astype(np.float32).astype(dtype).astype(np.float64)
    return np.moveaxis((codes * scale).reshape(v.shape), -1, axis)


WIDE = False


def mx_kscale(k):
    if not WIDE:
        return np.ones(k)
    levels = np.array([30, -30])
    if k % 512:
        return np.exp2(np.random.permutation(np.resize(levels, k // 32))).repeat(32)
    a = np.empty((k // 512, 16))
    for p in range(k // 512):
        a[p, :8] = np.random.permutation(np.resize(levels, 8))
        for g in range(8):
            far = levels[np.abs(levels - a[p, g]) >= 10]
            a[p, g + 8] = far[np.random.randint(len(far))]
    return np.exp2(a.ravel()).repeat(32)


def f64(x):
    return np.asarray(x).astype(np.float64)


def striped(idx):
    return np.tile(np.asarray(idx).reshape(-1, 16).T, (8, 1)).astype(np.uint16)


def unstriped(offs):
    return offs[:16].T.reshape(-1).astype(np.int64)


E2M1 = np.array([0.0, 0.5, 1.0, 1.5, 2.0, 3.0, 4.0, 6.0, -0.0, -0.5, -1.0, -1.5, -2.0, -3.0, -4.0, -6.0])


def pack_weight(w, fmt):
    k, n = w.shape
    w = f64(np.asarray(w, np.float32).astype(ml_dtypes.bfloat16)).reshape(k // 32, 32, n)
    amax = np.abs(w).max(1)
    if fmt in ("e4m3", "e5m2"):
        byte = np.frexp(amax)[1] - 1 + 127 - (7 if fmt == "e4m3" else 14)
    else:
        mant, ex = np.frexp(amax / 6.0)
        byte = np.where(mant > 0.5, ex, ex - 1) + 127
    byte = np.clip(np.where(amax > 0, byte, 1), 1, 254)
    scaled = (w * np.exp2(127.0 - byte)[:, None, :]).reshape(k, n).astype(np.float32)
    by_word = np.ascontiguousarray(scaled.reshape(k // 512, 128, 4, n).transpose(0, 1, 3, 2))
    if fmt in ("e4m3", "e5m2"):
        words = by_word.astype(ml_dtypes.float8_e4m3fn if fmt == "e4m3" else ml_dtypes.float8_e5m2).view(np.uint8)
    else:
        c = by_word.astype(ml_dtypes.float4_e2m1fn).view(np.uint8) & 0xF
        words = (c[..., 0::2] | (c[..., 1::2] << 4)).reshape(k // 512, 128, 2 * n)
    return np.ascontiguousarray(words), np.ascontiguousarray(byte.astype(np.uint8).reshape(k // 512, 16, n))


def unpack_weight(words, scales, fmt):
    g, _, n = scales.shape
    words = np.ascontiguousarray(words).reshape(g, 128, n, -1)
    if fmt in ("e4m3", "e5m2"):
        vals = words.view(ml_dtypes.float8_e4m3fn if fmt == "e4m3" else ml_dtypes.float8_e5m2).astype(np.float64)
    else:
        nib = np.empty((g, 128, n, 4), np.uint8)
        nib[..., 0::2] = words & 0xF
        nib[..., 1::2] = words >> 4
        vals = E2M1[nib]
    vals = vals * np.repeat(np.exp2(scales.astype(np.float64) - 127.0), 8, axis=1)[..., None]
    return vals.transpose(0, 1, 3, 2).reshape(g * 512, n)


K, T, Z, J, R, C, N, L, E = 512, 1024, 1024, 256, 512, 512, 256, 512, 1024


def setup_inputs():
    n = np.random.standard_normal
    idx = np.random.permutation(T)[:J]
    idx2 = np.random.permutation(Z)[:J]
    idx3 = np.random.permutation(C)[:J]
    idx4 = np.random.permutation(C)[:J]
    idx5 = np.random.permutation(E)[:J]
    fk = mx_kscale(K)
    fr = mx_kscale(R)
    fl = mx_kscale(L)
    xtp = pack_weight(n((K, T)) / fk[:, None], "e2m1")
    xop = pack_weight(n((K, Z)) / fk[:, None], "e5m2")
    wp = pack_weight(n((K, R)) * 1 / np.sqrt(K) * fk[:, None] * fr, "e5m2")
    wbp = pack_weight(n((R, N)) * 1 / np.sqrt(R) / fr[:, None], "e4m3")
    sxp = pack_weight(n((L, J)) / fl[:, None], "e5m2")
    wsp = pack_weight(n((L, N)) * 1 / np.sqrt(L) * fl[:, None], "e4m3")
    return {
        "xt_words": xtp[0],
        "xt_scales": xtp[1],
        "xo_words": xop[0],
        "xo_scales": xop[1],
        "w_words": wp[0],
        "w_scales": wp[1],
        "wb_words": wbp[0],
        "wb_scales": wbp[1],
        "sx_words": sxp[0],
        "sx_scales": sxp[1],
        "ws_words": wsp[0],
        "ws_scales": wsp[1],
        "offs": striped(idx),
        "offs2": striped(idx2),
        "offs3": striped(idx3),
        "offs4": striped(idx4),
        "offs5": striped(idx5),
    }


def reference(xt_words, xt_scales, xo_words, xo_scales, w_words, w_scales, wb_words, wb_scales, sx_words, sx_scales, ws_words, ws_scales, offs, offs2, offs3, offs4, offs5):
    idx = unstriped(offs)
    idx2 = unstriped(offs2)
    idx3 = unstriped(offs3)
    idx4 = unstriped(offs4)
    idx5 = unstriped(offs5)
    xtu = unpack_weight(xt_words, xt_scales, "e2m1")
    xou = unpack_weight(xo_words, xo_scales, "e5m2")
    wu = unpack_weight(w_words, w_scales, "e5m2")
    wbu = unpack_weight(wb_words, wb_scales, "e4m3")
    sxu = unpack_weight(sx_words, sx_scales, "e5m2")
    wsu = unpack_weight(ws_words, ws_scales, "e4m3")
    xtidxg = xtu[:, idx]
    a = wu.T @ xtidxg
    xoidx2g = xou[:, idx2]
    b = wu.T @ xoidx2g
    pw = np.zeros((R, C))
    pw[:, idx3] = a
    hid = np.maximum(pw[:, idx4], b)
    hidq = mxq(hid, 0, "e5m2")
    p = wbu.T @ hidq + wsu.T @ sxu
    y = np.zeros((N, E))
    y[:, idx5] = p
    return y

@@ -1,0 +1,171 @@
+from contextlib import ExitStack
+
+import concourse.mybir as mybir
+
+K, T, Z, J, R, C, N, L, E = 512, 1024, 1024, 256, 512, 512, 256, 512, 1024
+FLOPS = 2 * J * (2 * K * R + R * N + L * N)
+
+F32 = mybir.dt.float32
+BF16 = mybir.dt.bfloat16
+I32 = mybir.dt.int32
+U32 = mybir.dt.uint32
+U16 = mybir.dt.uint16
+U8 = mybir.dt.uint8
+E4M3 = mybir.dt.float8_e4m3fn_x4
+E5M2 = mybir.dt.float8_e5m2_x4
+E2M1 = mybir.dt.float4_e2m1fn_x4
+COPY = mybir.ActivationFunctionType.Copy
+MAX = mybir.AluOpType.max
+
+P = 128
+PACK = 4
+HALF = J // 2
+LIST_COLS = J // 16
+
+
+def load_words(queue, tile, words):
+    queue.dma_start(out=tile[:].bitcast(I32), in_=words[0].rearrange("p c r -> p (c r)").bitcast(I32))
+
+
+def load_scales(queue, plane, scales):
+    for q in range(4):
+        queue.dma_start(out=plane[32 * q : 32 * q + 4, :].bitcast(I32), in_=scales[0, 4 * q : 4 * q + 4, :].bitcast(I32))
+
+
+def tile_list_oneforboth_board_skip_scattered_kernel(
+    tc, xt_words, xt_scales, xo_words, xo_scales, w_words, w_scales, wb_words, wb_scales,
+    sx_words, sx_scales, ws_words, ws_scales, offs, offs2, offs3, offs4, offs5, out,
+):
+    nc = tc.nc
+    with ExitStack() as ctx:
+        keep = ctx.enter_context(tc.tile_pool(name="keep", bufs=1))
+        psum = ctx.enter_context(tc.psum_pool(name="psum", bufs=1))
+
+        def sb(shape, dtype, name, tag=None):
+            return keep.tile(shape, dtype, name=name, tag=tag or name, align_bytes=64)
+
+        tok_list = sb([P, LIST_COLS], U16, "tok_list")
+        note_list = sb([P, LIST_COLS], U16, "note_list")
+        put_list = sb([P, LIST_COLS], U16, "put_list")
+        read_list = sb([P, LIST_COLS], U16, "read_list")
+        page_list = sb([P, LIST_COLS], U16, "page_list")
+
+        xt_w = sb([P, T], U16, "xt_w")
+        xt_s = sb([P, T], U8, "xt_s")
+        xo_w = sb([P, Z], U32, "xo_w")
+        xo_s = sb([P, Z], U8, "xo_s")
+        w_w = sb([P, R], U32, "w_w", "slot0")
+        w_s = sb([P, R], U8, "w_s", "slot1")
+        wb_w = sb([P, N], U32, "wb_w")
+        ws_w = sb([P, N], U32, "ws_w")
+        sx_w = sb([P, J], U32, "sx_w")
+        late_s = sb([P, 2 * N + J], U8, "late_s")
+        wb_s, ws_s, sx_s = late_s[:, 0:N], late_s[:, N : 2 * N], late_s[:, 2 * N :]
+
+        boards = [sb([P, C], F32, f"board{t}") for t in range(PACK)]
+
+        for plane in (w_s, xt_s, xo_s, late_s):
+            nc.gpsimd.memset(plane[:].bitcast(I32), 0)
+        for t in range(PACK):
+            nc.vector.memset(boards[t][:], 0.0)
+
+        nc.sync.dma_start(out=tok_list[:], in_=offs)
+        load_words(nc.scalar, w_w, w_words)
+        nc.sync.dma_start(out=xt_w[:].bitcast(I32), in_=xt_words[0].bitcast(I32))
+        load_scales(nc.scalar, w_s, w_scales)
+        load_scales(nc.sync, xt_s, xt_scales)
+        nc.sync.dma_start(out=put_list[:], in_=offs3)
+        nc.sync.dma_start(out=note_list[:], in_=offs2)
+        load_words(nc.sync, xo_w, xo_words)
+        load_scales(nc.sync, xo_s, xo_scales)
+        nc.sync.dma_start(out=read_list[:], in_=offs4)
+        load_words(nc.sync, ws_w, ws_words)
+        load_words(nc.sync, sx_w, sx_words)
+        load_words(nc.sync, wb_w, wb_words)
+        load_scales(nc.sync, ws_s, ws_scales)
+        load_scales(nc.sync, sx_s, sx_scales)
+        load_scales(nc.sync, wb_s, wb_scales)
+        nc.sync.dma_start(out=page_list[:], in_=offs5)
+
+        wd_w = sb([P, PACK, P], U32, "wd_w")
+        wd_s = sb([P, PACK, P], U8, "wd_s")
+        nc.vector.tensor_copy(out=wd_w[:], in_=w_w[:].rearrange("p (q t) -> p t q", t=PACK))
+        tok_w = sb([P, J], U16, "tok_w")
+        tok_s = sb([P, J], U8, "tok_s")
+        nc.vector.tensor_copy(out=tok_w[:], in_=xt_w[:].indirect(tok_list[:]))
+        nc.vector.tensor_copy(out=wd_s[:], in_=w_s[:].rearrange("p (q t) -> p t q", t=PACK))
+        nc.vector.tensor_copy(out=tok_s[:], in_=xt_s[:].indirect(tok_list[:]))
+
+        pages = [sb([P, E], F32, f"page{m}", f"slot{m}") for m in range(2)]
+        for m in range(2):
+            nc.gpsimd.memset(pages[m][:], 0.0)
+
+        a_ps = [psum.tile([P, J], F32, name=f"a_ps{t}") for t in range(PACK)]
+        for t in range(PACK):
+            nc.tensor.matmul_mx(out=a_ps[t][:], lhsT=wd_w[:, t, :].bitcast(E5M2), lhsT_scale=wd_s[:, t, :],
+                                rhs=tok_w[:].bitcast(E2M1), rhs_scale=tok_s[:], start=True, stop=True)
+
+        note_w = sb([P, J], U32, "note_w")
+        note_s = sb([P, J], U8, "note_s")
+        nc.vector.tensor_copy(out=note_w[:], in_=xo_w[:].indirect(note_list[:]))
+        nc.vector.tensor_copy(out=note_s[:], in_=xo_s[:].indirect(note_list[:]))
+
+        halves = [slice(h * HALF, (h + 1) * HALF) for h in range(2)]
+        list_halves = [slice(h * LIST_COLS // 2, (h + 1) * LIST_COLS // 2) for h in range(2)]
+        b_ps = [psum.tile([P, PACK, HALF], F32, name=f"b_ps{h}") for h in range(2)]
+        for h in range(2):
+            for t in range(PACK):
+                nc.tensor.matmul_mx(out=b_ps[h][:, t, :], lhsT=wd_w[:, t, :].bitcast(E5M2), lhsT_scale=wd_s[:, t, :],
+                                    rhs=note_w[:, halves[h]].bitcast(E5M2), rhs_scale=note_s[:, halves[h]],
+                                    start=True, stop=True)
+
+        p_ps = [psum.tile([P, 2, HALF], F32, name=f"p_ps{h}") for h in range(2)]
+        rows = [slice(m * P, (m + 1) * P) for m in range(2)]
+        for h in range(2):
+            for m in range(2):
+                nc.tensor.matmul_mx(out=p_ps[h][:, m, :], lhsT=ws_w[:, rows[m]].bitcast(E4M3), lhsT_scale=ws_s[:, rows[m]],
+                                    rhs=sx_w[:, halves[h]].bitcast(E5M2), rhs_scale=sx_s[:, halves[h]],
+                                    start=(m == 0), stop=False)
+
+        a_sb = [sb([P, J], F32, f"a_sb{t}") for t in range(PACK)]
+        nc.scalar.copy(out=a_sb[0][:], in_=a_ps[0][:])
+        nc.scalar.copy(out=a_sb[1][:], in_=a_ps[1][:])
+        nc.scalar.activation(out=boards[0][:].indirect(put_list[:]), in_=a_sb[0][:], func=COPY)
+        nc.vector.tensor_copy(out=boards[1][:].indirect(put_list[:]), in_=a_sb[1][:])
+        nc.scalar.copy(out=a_sb[2][:], in_=a_ps[2][:])
+        nc.vector.tensor_copy(out=a_sb[3][:], in_=a_ps[3][:])
+        nc.scalar.activation(out=boards[2][:].indirect(put_list[:]), in_=a_sb[2][:], func=COPY)
+        nc.vector.tensor_copy(out=boards[3][:].indirect(put_list[:]), in_=a_sb[3][:])
+
+        read = [sb([P, PACK, HALF], F32, f"read{h}") for h in range(2)]
+        for t in range(PACK):
+            looked_up = boards[t][:].indirect(read_list[:, list_halves[0]])
+            if t % 2 == 0:
+                nc.scalar.activation(out=read[0][:, t, :], in_=looked_up, func=COPY)
+            else:
+                nc.vector.tensor_copy(out=read[0][:, t, :], in_=looked_up)
+        for t in range(PACK):
+            nc.scalar.activation(out=read[1][:, t, :], in_=boards[t][:].indirect(read_list[:, list_halves[1]]), func=COPY)
+
+        hid = [sb([P, HALF * PACK], BF16, f"hid{h}") for h in range(2)]
+        hid_w = [sb([P, HALF], U32, f"hid_w{h}") for h in range(2)]
+        hid_s = [sb([P, HALF], U8, f"hid_s{h}") for h in range(2)]
+        p_sb = [sb([P, 2, HALF], F32, f"p_sb{h}") for h in range(2)]
+        for h in range(2):
+            nc.vector.tensor_tensor(
+                out=hid[h][:].rearrange("p (c i t) -> p c t i", i=4, t=PACK),
+                in0=read[h][:].rearrange("p t (c i) -> p c t i", i=4),
+                in1=b_ps[h][:].rearrange("p t (c i) -> p c t i", i=4),
+                op=MAX,
+            )
+            nc.vector.quantize_mx(out=hid_w[h][:].bitcast(E5M2), scales=hid_s[h][:], in_=hid[h][:])
+            for m in range(2):
+                nc.tensor.matmul_mx(out=p_ps[h][:, m, :], lhsT=wb_w[:, rows[m]].bitcast(E4M3), lhsT_scale=wb_s[:, rows[m]],
+                                    rhs=hid_w[h][:].bitcast(E5M2), rhs_scale=hid_s[h][:],
+                                    start=False, stop=(m == 1))
+        for h in range(2):
+            nc.scalar.copy(out=p_sb[h][:], in_=p_ps[h][:])
+            nc.scalar.activation(out=pages[0][:].indirect(page_list[:, list_halves[h]]), in_=p_sb[h][:, 0, :], func=COPY)
+            nc.vector.tensor_copy(out=pages[1][:].indirect(page_list[:, list_halves[h]]), in_=p_sb[h][:, 1, :])
+        nc.scalar.dma_start(out=out[rows[0], :], in_=pages[0][:])
+        nc.sync.dma_start(out=out[rows[1], :], in_=pages[1][:])

@@ -27,8 +27,8 @@ def load_words(queue, tile, words):
     queue.dma_start(out=tile[:].bitcast(I32), in_=words[0].rearrange("p c r -> p (c r)").bitcast(I32))
 
 
-def load_scales(queue, plane, scales):
-    for q in range(4):
+def load_scales(queue, plane, scales, quadrants=range(4)):
+    for q in quadrants:
         queue.dma_start(out=plane[32 * q : 32 * q + 4, :].bitcast(I32), in_=scales[0, 4 * q : 4 * q + 4, :].bitcast(I32))
 
 
@@ -39,6 +39,8 @@ def tile_list_oneforboth_board_skip_scattered_kernel(
     nc = tc.nc
     with ExitStack() as ctx:
         keep = ctx.enter_context(tc.tile_pool(name="keep", bufs=1))
+        stage = ctx.enter_context(tc.tile_pool(name="stage", bufs=1))
+        reuse = ctx.enter_context(tc.tile_pool(name="reuse", bufs=1))
         psum = ctx.enter_context(tc.psum_pool(name="psum", bufs=1))
 
         def sb(shape, dtype, name, tag=None):
@@ -54,8 +56,8 @@ def tile_list_oneforboth_board_skip_scattered_kernel(
         xt_s = sb([P, T], U8, "xt_s")
         xo_w = sb([P, Z], U32, "xo_w")
         xo_s = sb([P, Z], U8, "xo_s")
-        w_w = sb([P, R], U32, "w_w", "slot0")
-        w_s = sb([P, R], U8, "w_s", "slot1")
+        w_w = sb([P, R], U32, "w_w")
+        w_s = reuse.tile([P, R], U8, name="w_s", offset=E * 4 - R // 2, align_bytes=64)
         wb_w = sb([P, N], U32, "wb_w")
         ws_w = sb([P, N], U32, "ws_w")
         sx_w = sb([P, J], U32, "sx_w")
@@ -64,16 +66,19 @@ def tile_list_oneforboth_board_skip_scattered_kernel(
 
         boards = [sb([P, C], F32, f"board{t}") for t in range(PACK)]
 
-        for plane in (w_s, xt_s, xo_s, late_s):
+        for plane in (xt_s, w_s):
             nc.gpsimd.memset(plane[:].bitcast(I32), 0)
+        for plane in (xo_s, late_s):
+            nc.vector.memset(plane[:].bitcast(I32), 0)
         for t in range(PACK):
             nc.vector.memset(boards[t][:], 0.0)
 
         nc.sync.dma_start(out=tok_list[:], in_=offs)
-        load_words(nc.scalar, w_w, w_words)
         nc.sync.dma_start(out=xt_w[:].bitcast(I32), in_=xt_words[0].bitcast(I32))
-        load_scales(nc.scalar, w_s, w_scales)
-        load_scales(nc.sync, xt_s, xt_scales)
+        load_scales(nc.sync, xt_s, xt_scales, range(1))
+        load_words(nc.sync, w_w, w_words)
+        load_scales(nc.sync, xt_s, xt_scales, range(1, 4))
+        load_scales(nc.sync, w_s, w_scales)
         nc.sync.dma_start(out=put_list[:], in_=offs3)
         nc.sync.dma_start(out=note_list[:], in_=offs2)
         load_words(nc.sync, xo_w, xo_words)
@@ -87,84 +92,108 @@ def tile_list_oneforboth_board_skip_scattered_kernel(
         load_scales(nc.sync, wb_s, wb_scales)
         nc.sync.dma_start(out=page_list[:], in_=offs5)
 
-        wd_w = sb([P, PACK, P], U32, "wd_w")
-        wd_s = sb([P, PACK, P], U8, "wd_s")
-        nc.vector.tensor_copy(out=wd_w[:], in_=w_w[:].rearrange("p (q t) -> p t q", t=PACK))
         tok_w = sb([P, J], U16, "tok_w")
         tok_s = sb([P, J], U8, "tok_s")
         nc.vector.tensor_copy(out=tok_w[:], in_=xt_w[:].indirect(tok_list[:]))
-        nc.vector.tensor_copy(out=wd_s[:], in_=w_s[:].rearrange("p (q t) -> p t q", t=PACK))
         nc.vector.tensor_copy(out=tok_s[:], in_=xt_s[:].indirect(tok_list[:]))
+        wd_w = sb([P, PACK, P], U32, "wd_w")
+        wd_s = [sb([P, P], U8, f"wd_s{t}") for t in range(PACK)]
+        nc.vector.tensor_copy(out=wd_w[:], in_=w_w[:].rearrange("p (q t) -> p t q", t=PACK))
+        for t in range(PACK):
+            nc.vector.tensor_copy(out=wd_s[t][:], in_=w_s[:, t::PACK])
 
-        pages = [sb([P, E], F32, f"page{m}", f"slot{m}") for m in range(2)]
+        pages = [reuse.tile([P, E], F32, name=f"page{m}", offset=m * E * 4) for m in range(2)]
         for m in range(2):
             nc.gpsimd.memset(pages[m][:], 0.0)
 
-        a_ps = [psum.tile([P, J], F32, name=f"a_ps{t}") for t in range(PACK)]
+        a_ps = [psum.tile([P, J], F32, name=f"a_ps{t}", tag=f"bank{t}") for t in range(PACK)]
         for t in range(PACK):
-            nc.tensor.matmul_mx(out=a_ps[t][:], lhsT=wd_w[:, t, :].bitcast(E5M2), lhsT_scale=wd_s[:, t, :],
+            nc.tensor.matmul_mx(out=a_ps[t][:], lhsT=wd_w[:, t, :].bitcast(E5M2), lhsT_scale=wd_s[t][:],
                                 rhs=tok_w[:].bitcast(E2M1), rhs_scale=tok_s[:], start=True, stop=True)
 
-        note_w = sb([P, J], U32, "note_w")
-        note_s = sb([P, J], U8, "note_s")
+        half_bytes = PACK * HALF * 4
+        a_last = stage.tile([P, 2, J], F32, name="a_last", offset=half_bytes // 2)
+        a_sb = [
+            stage.tile([P, J], F32, name="a_sb0", offset=2 * half_bytes + J // 2)[:],
+            sb([P, J], F32, "a_sb1")[:],
+            a_last[:, 0, :],
+            a_last[:, 1, :],
+        ]
+        for t in range(PACK):
+            nc.scalar.copy(out=a_sb[t], in_=a_ps[t][:])
+
+        def put(t):
+            if t % 2 == 1:
+                nc.scalar.activation(out=boards[t][:].indirect(put_list[:]), in_=a_sb[t], func=COPY)
+            else:
+                nc.vector.tensor_copy(out=boards[t][:].indirect(put_list[:]), in_=a_sb[t])
+
+        put(0)
+        put(1)
+
+        note_s = stage.tile([P, J], U8, name="note_s", offset=2 * half_bytes, align_bytes=64)
+        note_w = stage.tile([P, J], U32, name="note_w", offset=2 * half_bytes + J, align_bytes=64)
         nc.vector.tensor_copy(out=note_w[:], in_=xo_w[:].indirect(note_list[:]))
         nc.vector.tensor_copy(out=note_s[:], in_=xo_s[:].indirect(note_list[:]))
 
         halves = [slice(h * HALF, (h + 1) * HALF) for h in range(2)]
         list_halves = [slice(h * LIST_COLS // 2, (h + 1) * LIST_COLS // 2) for h in range(2)]
-        b_ps = [psum.tile([P, PACK, HALF], F32, name=f"b_ps{h}") for h in range(2)]
+        b_ps = [psum.tile([P, PACK, HALF], F32, name=f"b_ps{h}", tag=f"bank{h}") for h in range(2)]
         for h in range(2):
             for t in range(PACK):
-                nc.tensor.matmul_mx(out=b_ps[h][:, t, :], lhsT=wd_w[:, t, :].bitcast(E5M2), lhsT_scale=wd_s[:, t, :],
+                nc.tensor.matmul_mx(out=b_ps[h][:, t, :], lhsT=wd_w[:, t, :].bitcast(E5M2), lhsT_scale=wd_s[t][:],
                                     rhs=note_w[:, halves[h]].bitcast(E5M2), rhs_scale=note_s[:, halves[h]],
                                     start=True, stop=True)
 
-        p_ps = [psum.tile([P, 2, HALF], F32, name=f"p_ps{h}") for h in range(2)]
+        p_ps = [[psum.tile([P, HALF], F32, name=f"p_ps{h}{m}") for m in range(2)] for h in range(2)]
         rows = [slice(m * P, (m + 1) * P) for m in range(2)]
         for h in range(2):
             for m in range(2):
-                nc.tensor.matmul_mx(out=p_ps[h][:, m, :], lhsT=ws_w[:, rows[m]].bitcast(E4M3), lhsT_scale=ws_s[:, rows[m]],
+                nc.tensor.matmul_mx(out=p_ps[h][m][:], lhsT=ws_w[:, rows[m]].bitcast(E4M3), lhsT_scale=ws_s[:, rows[m]],
                                     rhs=sx_w[:, halves[h]].bitcast(E5M2), rhs_scale=sx_s[:, halves[h]],
-                                    start=(m == 0), stop=False)
+                                    start=True, stop=False)
 
-        a_sb = [sb([P, J], F32, f"a_sb{t}") for t in range(PACK)]
-        nc.scalar.copy(out=a_sb[0][:], in_=a_ps[0][:])
-        nc.scalar.copy(out=a_sb[1][:], in_=a_ps[1][:])
-        nc.scalar.activation(out=boards[0][:].indirect(put_list[:]), in_=a_sb[0][:], func=COPY)
-        nc.vector.tensor_copy(out=boards[1][:].indirect(put_list[:]), in_=a_sb[1][:])
-        nc.scalar.copy(out=a_sb[2][:], in_=a_ps[2][:])
-        nc.vector.tensor_copy(out=a_sb[3][:], in_=a_ps[3][:])
-        nc.scalar.activation(out=boards[2][:].indirect(put_list[:]), in_=a_sb[2][:], func=COPY)
-        nc.vector.tensor_copy(out=boards[3][:].indirect(put_list[:]), in_=a_sb[3][:])
+        put(2)
+        put(3)
 
-        read = [sb([P, PACK, HALF], F32, f"read{h}") for h in range(2)]
-        for t in range(PACK):
-            looked_up = boards[t][:].indirect(read_list[:, list_halves[0]])
-            if t % 2 == 0:
-                nc.scalar.activation(out=read[0][:, t, :], in_=looked_up, func=COPY)
+        read = [stage.tile([P, PACK, HALF], F32, name=f"read{h}", offset=h * half_bytes) for h in range(2)]
+
+        def look_up(h, t, on_vector):
+            looked_up = boards[t][:].indirect(read_list[:, list_halves[h]])
+            if on_vector:
+                nc.vector.tensor_copy(out=read[h][:, t, :], in_=looked_up)
             else:
-                nc.vector.tensor_copy(out=read[0][:, t, :], in_=looked_up)
-        for t in range(PACK):
-            nc.scalar.activation(out=read[1][:, t, :], in_=boards[t][:].indirect(read_list[:, list_halves[1]]), func=COPY)
+                nc.scalar.activation(out=read[h][:, t, :], in_=looked_up, func=COPY)
 
-        hid = [sb([P, HALF * PACK], BF16, f"hid{h}") for h in range(2)]
+        for t in range(PACK):
+            look_up(0, t, t % 2 == 0)
+        for t in range(1, PACK):
+            look_up(1, t, False)
+
+        hid = sb([P, HALF * PACK], BF16, "hid")
         hid_w = [sb([P, HALF], U32, f"hid_w{h}") for h in range(2)]
         hid_s = [sb([P, HALF], U8, f"hid_s{h}") for h in range(2)]
         p_sb = [sb([P, 2, HALF], F32, f"p_sb{h}") for h in range(2)]
         for h in range(2):
             nc.vector.tensor_tensor(
-                out=hid[h][:].rearrange("p (c i t) -> p c t i", i=4, t=PACK),
+                out=hid[:].rearrange("p (c i t) -> p c t i", i=4, t=PACK),
                 in0=read[h][:].rearrange("p t (c i) -> p c t i", i=4),
                 in1=b_ps[h][:].rearrange("p t (c i) -> p c t i", i=4),
                 op=MAX,
             )
-            nc.vector.quantize_mx(out=hid_w[h][:].bitcast(E5M2), scales=hid_s[h][:], in_=hid[h][:])
+            if h == 0:
+                look_up(1, 0, True)
+            nc.vector.quantize_mx(out=hid_w[h][:].bitcast(E5M2), scales=hid_s[h][:], in_=hid[:])
             for m in range(2):
-                nc.tensor.matmul_mx(out=p_ps[h][:, m, :], lhsT=wb_w[:, rows[m]].bitcast(E4M3), lhsT_scale=wb_s[:, rows[m]],
+                nc.tensor.matmul_mx(out=p_ps[h][m][:], lhsT=wb_w[:, rows[m]].bitcast(E4M3), lhsT_scale=wb_s[:, rows[m]],
                                     rhs=hid_w[h][:].bitcast(E5M2), rhs_scale=hid_s[h][:],
-                                    start=False, stop=(m == 1))
+                                    start=False, stop=True)
         for h in range(2):
-            nc.scalar.copy(out=p_sb[h][:], in_=p_ps[h][:])
+            nc.scalar.copy(out=p_sb[h][:, 0, :], in_=p_ps[h][0][:])
+            if h == 0:
+                nc.scalar.copy(out=p_sb[h][:, 1, :], in_=p_ps[h][1][:])
+            else:
+                nc.vector.tensor_copy(out=p_sb[h][:, 1, :], in_=p_ps[h][1][:])
             nc.scalar.activation(out=pages[0][:].indirect(page_list[:, list_halves[h]]), in_=p_sb[h][:, 0, :], func=COPY)
             nc.vector.tensor_copy(out=pages[1][:].indirect(page_list[:, list_halves[h]]), in_=p_sb[h][:, 1, :])
         nc.scalar.dma_start(out=out[rows[0], :], in_=pages[0][:])

@@ -21,15 +21,26 @@ P = 128
 PACK = 4
 HALF = J // 2
 LIST_COLS = J // 16
+F32_BYTES = 4
+RUN = 4
 
 
-def load_words(queue, tile, words):
-    queue.dma_start(out=tile[:].bitcast(I32), in_=words[0].rearrange("p c r -> p (c r)").bitcast(I32))
+def load_words(nc, tile, words):
+    nc.sync.dma_start(out=tile[:].bitcast(I32), in_=words[0].rearrange("p c r -> p (c r)").bitcast(I32))
 
 
-def load_scales(queue, plane, scales, quadrants=range(4)):
+def load_scales(nc, plane, scales, quadrants=range(4)):
     for q in quadrants:
-        queue.dma_start(out=plane[32 * q : 32 * q + 4, :].bitcast(I32), in_=scales[0, 4 * q : 4 * q + 4, :].bitcast(I32))
+        nc.sync.dma_start(
+            out=plane[32 * q : 32 * q + 4, :].bitcast(I32), in_=scales[0, 4 * q : 4 * q + 4, :].bitcast(I32)
+        )
+
+
+def move(nc, on_vector, out, in_):
+    if on_vector:
+        nc.vector.tensor_copy(out=out, in_=in_)
+    else:
+        nc.scalar.activation(out=out, in_=in_, func=COPY)
 
 
 def tile_list_oneforboth_board_skip_scattered_kernel(
@@ -40,11 +51,11 @@ def tile_list_oneforboth_board_skip_scattered_kernel(
     with ExitStack() as ctx:
         keep = ctx.enter_context(tc.tile_pool(name="keep", bufs=1))
         stage = ctx.enter_context(tc.tile_pool(name="stage", bufs=1))
-        reuse = ctx.enter_context(tc.tile_pool(name="reuse", bufs=1))
+        paging = ctx.enter_context(tc.tile_pool(name="paging", bufs=1))
         psum = ctx.enter_context(tc.psum_pool(name="psum", bufs=1))
 
-        def sb(shape, dtype, name, tag=None):
-            return keep.tile(shape, dtype, name=name, tag=tag or name, align_bytes=64)
+        def sb(shape, dtype, name):
+            return keep.tile(shape, dtype, name=name, align_bytes=64)
 
         tok_list = sb([P, LIST_COLS], U16, "tok_list")
         note_list = sb([P, LIST_COLS], U16, "note_list")
@@ -52,12 +63,14 @@ def tile_list_oneforboth_board_skip_scattered_kernel(
         read_list = sb([P, LIST_COLS], U16, "read_list")
         page_list = sb([P, LIST_COLS], U16, "page_list")
 
+        half_bytes = PACK * HALF * F32_BYTES
+        page_bytes = E * F32_BYTES
         xt_w = sb([P, T], U16, "xt_w")
         xt_s = sb([P, T], U8, "xt_s")
         xo_w = sb([P, Z], U32, "xo_w")
-        xo_s = sb([P, Z], U8, "xo_s")
+        xo_s = stage.tile([P, Z], U8, name="xo_s", offset=2 * half_bytes - Z, align_bytes=64)
         w_w = sb([P, R], U32, "w_w")
-        w_s = reuse.tile([P, R], U8, name="w_s", offset=E * 4 - R // 2, align_bytes=64)
+        w_s = paging.tile([P, R], U8, name="w_s", offset=page_bytes - R // 2, align_bytes=64)
         wb_w = sb([P, N], U32, "wb_w")
         ws_w = sb([P, N], U32, "ws_w")
         sx_w = sb([P, J], U32, "sx_w")
@@ -75,73 +88,68 @@ def tile_list_oneforboth_board_skip_scattered_kernel(
 
         nc.sync.dma_start(out=tok_list[:], in_=offs)
         nc.sync.dma_start(out=xt_w[:].bitcast(I32), in_=xt_words[0].bitcast(I32))
-        load_scales(nc.sync, xt_s, xt_scales, range(1))
-        load_words(nc.sync, w_w, w_words)
-        load_scales(nc.sync, xt_s, xt_scales, range(1, 4))
-        load_scales(nc.sync, w_s, w_scales)
+        load_scales(nc, xt_s, xt_scales, range(1))
+        load_words(nc, w_w, w_words)
+        load_scales(nc, xt_s, xt_scales, range(1, 4))
+        load_scales(nc, w_s, w_scales)
         nc.sync.dma_start(out=put_list[:], in_=offs3)
+        load_words(nc, xo_w, xo_words)
+        load_scales(nc, xo_s, xo_scales)
         nc.sync.dma_start(out=note_list[:], in_=offs2)
-        load_words(nc.sync, xo_w, xo_words)
-        load_scales(nc.sync, xo_s, xo_scales)
         nc.sync.dma_start(out=read_list[:], in_=offs4)
-        load_words(nc.sync, ws_w, ws_words)
-        load_words(nc.sync, sx_w, sx_words)
-        load_words(nc.sync, wb_w, wb_words)
-        load_scales(nc.sync, ws_s, ws_scales)
-        load_scales(nc.sync, sx_s, sx_scales)
-        load_scales(nc.sync, wb_s, wb_scales)
+        load_words(nc, ws_w, ws_words)
+        load_words(nc, sx_w, sx_words)
+        load_words(nc, wb_w, wb_words)
+        load_scales(nc, ws_s, ws_scales)
+        load_scales(nc, sx_s, sx_scales)
+        load_scales(nc, wb_s, wb_scales)
         nc.sync.dma_start(out=page_list[:], in_=offs5)
 
         tok_w = sb([P, J], U16, "tok_w")
         tok_s = sb([P, J], U8, "tok_s")
         nc.vector.tensor_copy(out=tok_w[:], in_=xt_w[:].indirect(tok_list[:]))
         nc.vector.tensor_copy(out=tok_s[:], in_=xt_s[:].indirect(tok_list[:]))
-        wd_w = sb([P, PACK, P], U32, "wd_w")
-        wd_s = [sb([P, P], U8, f"wd_s{t}") for t in range(PACK)]
-        nc.vector.tensor_copy(out=wd_w[:], in_=w_w[:].rearrange("p (q t) -> p t q", t=PACK))
-        for t in range(PACK):
-            nc.vector.tensor_copy(out=wd_s[t][:], in_=w_s[:, t::PACK])
 
-        pages = [reuse.tile([P, E], F32, name=f"page{m}", offset=m * E * 4) for m in range(2)]
+        dealt_w = sb([P, PACK, P], U32, "dealt_w")
+        dealt_s = [sb([P, P], U8, f"dealt_s{t}") for t in range(PACK)]
+        nc.vector.tensor_copy(out=dealt_w[:], in_=w_w[:].rearrange("p (q t) -> p t q", t=PACK))
+        for t in range(PACK):
+            nc.vector.tensor_copy(out=dealt_s[t][:], in_=w_s[:, t::PACK])
+
+        pages = [paging.tile([P, E], F32, name=f"page{m}", offset=m * page_bytes) for m in range(2)]
         for m in range(2):
             nc.gpsimd.memset(pages[m][:], 0.0)
 
         a_ps = [psum.tile([P, J], F32, name=f"a_ps{t}", tag=f"bank{t}") for t in range(PACK)]
         for t in range(PACK):
-            nc.tensor.matmul_mx(out=a_ps[t][:], lhsT=wd_w[:, t, :].bitcast(E5M2), lhsT_scale=wd_s[t][:],
+            nc.tensor.matmul_mx(out=a_ps[t][:], lhsT=dealt_w[:, t, :].bitcast(E5M2), lhsT_scale=dealt_s[t][:],
                                 rhs=tok_w[:].bitcast(E2M1), rhs_scale=tok_s[:], start=True, stop=True)
 
-        half_bytes = PACK * HALF * 4
-        a_last = stage.tile([P, 2, J], F32, name="a_last", offset=half_bytes // 2)
         a_sb = [
-            stage.tile([P, J], F32, name="a_sb0", offset=2 * half_bytes + J // 2)[:],
-            sb([P, J], F32, "a_sb1")[:],
-            a_last[:, 0, :],
-            a_last[:, 1, :],
+            stage.tile([P, J], F32, name="a_sb0", offset=2 * half_bytes + J // 2),
+            sb([P, J], F32, "a_sb1"),
+            sb([P, J], F32, "a_sb2"),
+            stage.tile([P, J], F32, name="a_sb3", offset=half_bytes - J * F32_BYTES // 2),
         ]
         for t in range(PACK):
-            nc.scalar.copy(out=a_sb[t], in_=a_ps[t][:])
+            nc.scalar.copy(out=a_sb[t][:], in_=a_ps[t][:])
 
         def put(t):
-            if t % 2 == 1:
-                nc.scalar.activation(out=boards[t][:].indirect(put_list[:]), in_=a_sb[t], func=COPY)
-            else:
-                nc.vector.tensor_copy(out=boards[t][:].indirect(put_list[:]), in_=a_sb[t])
+            move(nc, t % 2 == 0, boards[t][:].indirect(put_list[:]), a_sb[t][:])
 
         put(0)
         put(1)
 
         note_s = stage.tile([P, J], U8, name="note_s", offset=2 * half_bytes, align_bytes=64)
         note_w = stage.tile([P, J], U32, name="note_w", offset=2 * half_bytes + J, align_bytes=64)
-        nc.vector.tensor_copy(out=note_w[:], in_=xo_w[:].indirect(note_list[:]))
-        nc.vector.tensor_copy(out=note_s[:], in_=xo_s[:].indirect(note_list[:]))
-
         halves = [slice(h * HALF, (h + 1) * HALF) for h in range(2)]
         list_halves = [slice(h * LIST_COLS // 2, (h + 1) * LIST_COLS // 2) for h in range(2)]
         b_ps = [psum.tile([P, PACK, HALF], F32, name=f"b_ps{h}", tag=f"bank{h}") for h in range(2)]
         for h in range(2):
+            nc.vector.tensor_copy(out=note_w[:, halves[h]], in_=xo_w[:].indirect(note_list[:, list_halves[h]]))
+            nc.vector.tensor_copy(out=note_s[:, halves[h]], in_=xo_s[:].indirect(note_list[:, list_halves[h]]))
             for t in range(PACK):
-                nc.tensor.matmul_mx(out=b_ps[h][:, t, :], lhsT=wd_w[:, t, :].bitcast(E5M2), lhsT_scale=wd_s[t][:],
+                nc.tensor.matmul_mx(out=b_ps[h][:, t, :], lhsT=dealt_w[:, t, :].bitcast(E5M2), lhsT_scale=dealt_s[t][:],
                                     rhs=note_w[:, halves[h]].bitcast(E5M2), rhs_scale=note_s[:, halves[h]],
                                     start=True, stop=True)
 
@@ -157,44 +165,32 @@ def tile_list_oneforboth_board_skip_scattered_kernel(
         put(3)
 
         read = [stage.tile([P, PACK, HALF], F32, name=f"read{h}", offset=h * half_bytes) for h in range(2)]
+        for h in range(2):
+            for t in range(PACK):
+                move(nc, h == 1 and t % 2 == 0, read[h][:, t, :], boards[t][:].indirect(read_list[:, list_halves[h]]))
 
-        def look_up(h, t, on_vector):
-            looked_up = boards[t][:].indirect(read_list[:, list_halves[h]])
-            if on_vector:
-                nc.vector.tensor_copy(out=read[h][:, t, :], in_=looked_up)
-            else:
-                nc.scalar.activation(out=read[h][:, t, :], in_=looked_up, func=COPY)
-
-        for t in range(PACK):
-            look_up(0, t, t % 2 == 0)
-        for t in range(1, PACK):
-            look_up(1, t, False)
-
-        hid = sb([P, HALF * PACK], BF16, "hid")
+        hid = [sb([P, HALF * PACK], BF16, f"hid{h}") for h in range(2)]
         hid_w = [sb([P, HALF], U32, f"hid_w{h}") for h in range(2)]
         hid_s = [sb([P, HALF], U8, f"hid_s{h}") for h in range(2)]
         p_sb = [sb([P, 2, HALF], F32, f"p_sb{h}") for h in range(2)]
         for h in range(2):
             nc.vector.tensor_tensor(
-                out=hid[:].rearrange("p (c i t) -> p c t i", i=4, t=PACK),
-                in0=read[h][:].rearrange("p t (c i) -> p c t i", i=4),
-                in1=b_ps[h][:].rearrange("p t (c i) -> p c t i", i=4),
+                out=hid[h][:].rearrange("p (c i t) -> p c t i", i=RUN, t=PACK),
+                in0=read[h][:].rearrange("p t (c i) -> p c t i", i=RUN),
+                in1=b_ps[h][:].rearrange("p t (c i) -> p c t i", i=RUN),
                 op=MAX,
             )
-            if h == 0:
-                look_up(1, 0, True)
-            nc.vector.quantize_mx(out=hid_w[h][:].bitcast(E5M2), scales=hid_s[h][:], in_=hid[:])
+            nc.vector.quantize_mx(out=hid_w[h][:].bitcast(E5M2), scales=hid_s[h][:], in_=hid[h][:])
             for m in range(2):
                 nc.tensor.matmul_mx(out=p_ps[h][m][:], lhsT=wb_w[:, rows[m]].bitcast(E4M3), lhsT_scale=wb_s[:, rows[m]],
                                     rhs=hid_w[h][:].bitcast(E5M2), rhs_scale=hid_s[h][:],
                                     start=False, stop=True)
+
         for h in range(2):
             nc.scalar.copy(out=p_sb[h][:, 0, :], in_=p_ps[h][0][:])
-            if h == 0:
-                nc.scalar.copy(out=p_sb[h][:, 1, :], in_=p_ps[h][1][:])
-            else:
-                nc.vector.tensor_copy(out=p_sb[h][:, 1, :], in_=p_ps[h][1][:])
-            nc.scalar.activation(out=pages[0][:].indirect(page_list[:, list_halves[h]]), in_=p_sb[h][:, 0, :], func=COPY)
-            nc.vector.tensor_copy(out=pages[1][:].indirect(page_list[:, list_halves[h]]), in_=p_sb[h][:, 1, :])
+            nc.vector.tensor_copy(out=p_sb[h][:, 1, :], in_=p_ps[h][1][:])
+        for h in range(2):
+            for m in range(2):
+                move(nc, m == 1, pages[m][:].indirect(page_list[:, list_halves[h]]), p_sb[h][:, m, :])
         nc.scalar.dma_start(out=out[rows[0], :], in_=pages[0][:])
         nc.sync.dma_start(out=out[rows[1], :], in_=pages[1][:])

from contextlib import ExitStack

import concourse.mybir as mybir

K, T, Z, J, R, C, N, L, E = 512, 1024, 1024, 256, 512, 512, 256, 512, 1024
FLOPS = 2 * J * (2 * K * R + R * N + L * N)

F32 = mybir.dt.float32
BF16 = mybir.dt.bfloat16
I32 = mybir.dt.int32
U32 = mybir.dt.uint32
U16 = mybir.dt.uint16
U8 = mybir.dt.uint8
E4M3 = mybir.dt.float8_e4m3fn_x4
E5M2 = mybir.dt.float8_e5m2_x4
E2M1 = mybir.dt.float4_e2m1fn_x4
COPY = mybir.ActivationFunctionType.Copy
MAX = mybir.AluOpType.max

P = 128
PACK = 4
HALF = J // 2
LIST_COLS = J // 16
F32_BYTES = 4
RUN = 4


def load_words(nc, tile, words):
    nc.sync.dma_start(out=tile[:].bitcast(I32), in_=words[0].rearrange("p c r -> p (c r)").bitcast(I32))


def load_scales(nc, plane, scales, quadrants=range(4)):
    for q in quadrants:
        nc.sync.dma_start(
            out=plane[32 * q : 32 * q + 4, :].bitcast(I32), in_=scales[0, 4 * q : 4 * q + 4, :].bitcast(I32)
        )


def move(nc, on_vector, out, in_):
    if on_vector:
        nc.vector.tensor_copy(out=out, in_=in_)
    else:
        nc.scalar.activation(out=out, in_=in_, func=COPY)


def tile_list_oneforboth_board_skip_scattered_kernel(
    tc, xt_words, xt_scales, xo_words, xo_scales, w_words, w_scales, wb_words, wb_scales,
    sx_words, sx_scales, ws_words, ws_scales, offs, offs2, offs3, offs4, offs5, out,
):
    nc = tc.nc
    with ExitStack() as ctx:
        keep = ctx.enter_context(tc.tile_pool(name="keep", bufs=1))
        stage = ctx.enter_context(tc.tile_pool(name="stage", bufs=1))
        paging = ctx.enter_context(tc.tile_pool(name="paging", bufs=1))
        psum = ctx.enter_context(tc.psum_pool(name="psum", bufs=1))

        def sb(shape, dtype, name):
            return keep.tile(shape, dtype, name=name, align_bytes=64)

        tok_list = sb([P, LIST_COLS], U16, "tok_list")
        note_list = sb([P, LIST_COLS], U16, "note_list")
        put_list = sb([P, LIST_COLS], U16, "put_list")
        read_list = sb([P, LIST_COLS], U16, "read_list")
        page_list = sb([P, LIST_COLS], U16, "page_list")

        half_bytes = PACK * HALF * F32_BYTES
        page_bytes = E * F32_BYTES
        xt_w = sb([P, T], U16, "xt_w")
        xt_s = sb([P, T], U8, "xt_s")
        xo_w = sb([P, Z], U32, "xo_w")
        xo_s = stage.tile([P, Z], U8, name="xo_s", offset=2 * half_bytes - Z, align_bytes=64)
        w_w = sb([P, R], U32, "w_w")
        w_s = paging.tile([P, R], U8, name="w_s", offset=page_bytes - R // 2, align_bytes=64)
        wb_w = sb([P, N], U32, "wb_w")
        ws_w = sb([P, N], U32, "ws_w")
        sx_w = sb([P, J], U32, "sx_w")
        late_s = sb([P, 2 * N + J], U8, "late_s")
        wb_s, ws_s, sx_s = late_s[:, 0:N], late_s[:, N : 2 * N], late_s[:, 2 * N :]

        boards = [sb([P, C], F32, f"board{t}") for t in range(PACK)]

        for plane in (xt_s, w_s):
            nc.gpsimd.memset(plane[:].bitcast(I32), 0)
        for plane in (xo_s, late_s):
            nc.vector.memset(plane[:].bitcast(I32), 0)
        for t in range(PACK):
            nc.vector.memset(boards[t][:], 0.0)

        nc.sync.dma_start(out=tok_list[:], in_=offs)
        nc.sync.dma_start(out=xt_w[:].bitcast(I32), in_=xt_words[0].bitcast(I32))
        load_scales(nc, xt_s, xt_scales, range(1))
        load_words(nc, w_w, w_words)
        load_scales(nc, xt_s, xt_scales, range(1, 4))
        load_scales(nc, w_s, w_scales)
        nc.sync.dma_start(out=put_list[:], in_=offs3)
        load_words(nc, xo_w, xo_words)
        load_scales(nc, xo_s, xo_scales)
        nc.sync.dma_start(out=note_list[:], in_=offs2)
        nc.sync.dma_start(out=read_list[:], in_=offs4)
        load_words(nc, ws_w, ws_words)
        load_words(nc, sx_w, sx_words)
        load_words(nc, wb_w, wb_words)
        load_scales(nc, ws_s, ws_scales)
        load_scales(nc, sx_s, sx_scales)
        load_scales(nc, wb_s, wb_scales)
        nc.sync.dma_start(out=page_list[:], in_=offs5)

        tok_w = sb([P, J], U16, "tok_w")
        tok_s = sb([P, J], U8, "tok_s")
        nc.vector.tensor_copy(out=tok_w[:], in_=xt_w[:].indirect(tok_list[:]))
        nc.vector.tensor_copy(out=tok_s[:], in_=xt_s[:].indirect(tok_list[:]))

        dealt_w = sb([P, PACK, P], U32, "dealt_w")
        dealt_s = [sb([P, P], U8, f"dealt_s{t}") for t in range(PACK)]
        nc.vector.tensor_copy(out=dealt_w[:], in_=w_w[:].rearrange("p (q t) -> p t q", t=PACK))
        for t in range(PACK):
            nc.vector.tensor_copy(out=dealt_s[t][:], in_=w_s[:, t::PACK])

        pages = [paging.tile([P, E], F32, name=f"page{m}", offset=m * page_bytes) for m in range(2)]
        for m in range(2):
            nc.gpsimd.memset(pages[m][:], 0.0)

        a_ps = [psum.tile([P, J], F32, name=f"a_ps{t}", tag=f"bank{t}") for t in range(PACK)]
        for t in range(PACK):
            nc.tensor.matmul_mx(out=a_ps[t][:], lhsT=dealt_w[:, t, :].bitcast(E5M2), lhsT_scale=dealt_s[t][:],
                                rhs=tok_w[:].bitcast(E2M1), rhs_scale=tok_s[:], start=True, stop=True)

        a_sb = [
            stage.tile([P, J], F32, name="a_sb0", offset=2 * half_bytes + J // 2),
            sb([P, J], F32, "a_sb1"),
            sb([P, J], F32, "a_sb2"),
            stage.tile([P, J], F32, name="a_sb3", offset=half_bytes - J * F32_BYTES // 2),
        ]
        for t in range(PACK):
            nc.scalar.copy(out=a_sb[t][:], in_=a_ps[t][:])

        def put(t):
            move(nc, t % 2 == 0, boards[t][:].indirect(put_list[:]), a_sb[t][:])

        put(0)
        put(1)

        note_s = stage.tile([P, J], U8, name="note_s", offset=2 * half_bytes, align_bytes=64)
        note_w = stage.tile([P, J], U32, name="note_w", offset=2 * half_bytes + J, align_bytes=64)
        halves = [slice(h * HALF, (h + 1) * HALF) for h in range(2)]
        list_halves = [slice(h * LIST_COLS // 2, (h + 1) * LIST_COLS // 2) for h in range(2)]
        b_ps = [psum.tile([P, PACK, HALF], F32, name=f"b_ps{h}", tag=f"bank{h}") for h in range(2)]
        for h in range(2):
            nc.vector.tensor_copy(out=note_w[:, halves[h]], in_=xo_w[:].indirect(note_list[:, list_halves[h]]))
            nc.vector.tensor_copy(out=note_s[:, halves[h]], in_=xo_s[:].indirect(note_list[:, list_halves[h]]))
            for t in range(PACK):
                nc.tensor.matmul_mx(out=b_ps[h][:, t, :], lhsT=dealt_w[:, t, :].bitcast(E5M2), lhsT_scale=dealt_s[t][:],
                                    rhs=note_w[:, halves[h]].bitcast(E5M2), rhs_scale=note_s[:, halves[h]],
                                    start=True, stop=True)

        p_ps = [[psum.tile([P, HALF], F32, name=f"p_ps{h}{m}") for m in range(2)] for h in range(2)]
        rows = [slice(m * P, (m + 1) * P) for m in range(2)]
        for h in range(2):
            for m in range(2):
                nc.tensor.matmul_mx(out=p_ps[h][m][:], lhsT=ws_w[:, rows[m]].bitcast(E4M3), lhsT_scale=ws_s[:, rows[m]],
                                    rhs=sx_w[:, halves[h]].bitcast(E5M2), rhs_scale=sx_s[:, halves[h]],
                                    start=True, stop=False)

        put(2)
        put(3)

        read = [stage.tile([P, PACK, HALF], F32, name=f"read{h}", offset=h * half_bytes) for h in range(2)]
        for h in range(2):
            for t in range(PACK):
                move(nc, h == 1 and t % 2 == 0, read[h][:, t, :], boards[t][:].indirect(read_list[:, list_halves[h]]))

        hid = [sb([P, HALF * PACK], BF16, f"hid{h}") for h in range(2)]
        hid_w = [sb([P, HALF], U32, f"hid_w{h}") for h in range(2)]
        hid_s = [sb([P, HALF], U8, f"hid_s{h}") for h in range(2)]
        p_sb = [sb([P, 2, HALF], F32, f"p_sb{h}") for h in range(2)]
        for h in range(2):
            nc.vector.tensor_tensor(
                out=hid[h][:].rearrange("p (c i t) -> p c t i", i=RUN, t=PACK),
                in0=read[h][:].rearrange("p t (c i) -> p c t i", i=RUN),
                in1=b_ps[h][:].rearrange("p t (c i) -> p c t i", i=RUN),
                op=MAX,
            )
            nc.vector.quantize_mx(out=hid_w[h][:].bitcast(E5M2), scales=hid_s[h][:], in_=hid[h][:])
            for m in range(2):
                nc.tensor.matmul_mx(out=p_ps[h][m][:], lhsT=wb_w[:, rows[m]].bitcast(E4M3), lhsT_scale=wb_s[:, rows[m]],
                                    rhs=hid_w[h][:].bitcast(E5M2), rhs_scale=hid_s[h][:],
                                    start=False, stop=True)

        for h in range(2):
            nc.scalar.copy(out=p_sb[h][:, 0, :], in_=p_ps[h][0][:])
            nc.vector.tensor_copy(out=p_sb[h][:, 1, :], in_=p_ps[h][1][:])
        for h in range(2):
            for m in range(2):
                move(nc, m == 1, pages[m][:].indirect(page_list[:, list_halves[h]]), p_sb[h][:, m, :])
        nc.scalar.dma_start(out=out[rows[0], :], in_=pages[0][:])
        nc.sync.dma_start(out=out[rows[1], :], in_=pages[1][:])
